import numpy as np, ml_dtypes
CORES = [52,68,84,180,196,212,308,324,340]
N = 9
F = 256
def setup_inputs(rng):
    m = (rng.standard_normal((N, 128, 128), dtype=np.float32) / 11).astype(ml_dtypes.bfloat16)
    return {"m": m, "mt": m.transpose(0, 2, 1).copy(), "x": rng.standard_normal((N, 128, F), dtype=np.float32).astype(ml_dtypes.bfloat16)}
def setup_inputs_big(rng):
    d = setup_inputs(rng)
    for k in ("x",): d[k] = (d[k].astype(np.float32) * 1048576.0).astype(d[k].dtype)
    return d
def setup_inputs_small(rng):
    d = setup_inputs(rng)
    for k in ("x",): d[k] = (d[k].astype(np.float32) * (1 / 1048576.0)).astype(d[k].dtype)
    return d
def setup_inputs_apart(rng):
    d = setup_inputs(rng)
    f = (10.0 ** rng.permutation(np.linspace(-1.5, 1.5, N))).astype(np.float32).reshape(N, 1, 1)
    for k in ("x",): d[k] = (d[k].astype(np.float32) * f).astype(d[k].dtype)
    return d
def reference(m, mt, x):
    M, X = m.astype(np.float64), x.astype(np.float64)
    y = np.zeros((N, 128, F)); p = X[0]
    for r in range(N):
        p = M[r].T @ p
        y[r] = p
    return {"y": y.astype(ml_dtypes.bfloat16)}

@@ -1,0 +1,181 @@
+from concourse.bass import DstId, RemoteDMATransfer
+
+F = 256
+_B = "bfloat16"
+SCRATCH = {
+    "sm": ("sbuf", [128, 128], _B), "smt": ("sbuf", [128, 128], _B), "sx": ("sbuf", [128, F], _B),
+    "pin": ("sbuf", [128, F], _B), "pout": ("sbuf", [128, F], _B), "yb": ("sbuf", [128, F], _B),
+    "LB": ("sbuf", [128, 128], _B),
+}
+for _j in range(1, 8):
+    SCRATCH["L%d" % _j] = ("sbuf", [128, 128], _B)
+for _j in range(6):
+    SCRATCH["t%d" % _j] = ("sbuf", [128, 128], _B)
+for _j in range(8):
+    SCRATCH["ps%d" % _j] = ("psum", [128, 512], "float32")
+
+SEMAPHORES = (["ld_sm", "ld_smt", "ld_sx", "a_pin", "a_LB", "sent", "st"] + ["a_L%d" % j for j in range(1, 8)]
+              + ["q%d" % j for j in range(8)] + ["c%d" % j for j in range(8)])
+
+
+def rank_program(g, core, T, topo):
+    rank = T.rank_of(core)
+    if rank is None:
+        return
+    cores = list(T.cores)
+    n = len(cores)
+    far = [r for r in range(1, n) if not topo.may_write(cores[0], cores[r])]
+    mid = [r for r in range(1, n) if r not in far and all(topo.may_write(cores[r], cores[f]) for f in far)]
+    third, pb, pa = mid[0], mid[1], mid[2]
+
+    def partner(r):
+        return [f for f in far if topo.chip(cores[f]) == topo.chip(cores[r])][0]
+    fa, fb, fc = partner(third), partner(pa), partner(pb)
+
+    Q = {"g": g, "t": g.tensor, "v": g.vector, "s": g.sync, "a": g.scalar}
+    seen, ready, cnt = {}, {}, {"mm": 0, "sent": 0}
+
+    def need(q, bufs):
+        for b in bufs:
+            s, v = ready[b]
+            if seen.get((q, s), 0) < v:
+                Q[q].wait_ge(T.sem[s], v)
+                seen[(q, s)] = v
+
+    def engines(mask):
+        return bin(mask).count("1")
+
+    def load(q, buf, src):
+        Q[q].dma_start(T[buf][:], src[:]).then_inc(T.sem["ld_" + buf], 16)
+        ready[buf] = ("ld_" + buf, 16)
+
+    def expect(buf, src_rank):
+        ready[buf] = ("a_" + buf, engines(topo.mask(cores[src_rank], core)))
+
+    def mm(out, lhsT, rhs):
+        k = cnt["mm"]
+        cnt["mm"] += 1
+        w = T[rhs].shape[1]
+        ps = T["ps%d" % k]
+        need("t", [lhsT, rhs])
+        g.tensor.matmul(ps[:, 0:w], T[lhsT][:], T[rhs][:], start=True, stop=True).then_inc(T.sem["q%d" % k], 1)
+        g.vector.wait_ge(T.sem["q%d" % k], 1)
+        g.vector.tensor_copy(T[out][:], ps[:, 0:w]).then_inc(T.sem["c%d" % k], 1)
+        ready[out] = ("c%d" % k, 1)
+
+    def send(buf, dst_buf, dsts):
+        need("g", [buf])
+        mask = topo.mask(core, cores[dsts[0]])
+        for d in dsts:
+            mask &= topo.mask(core, cores[d])
+        cnt["sent"] += engines(mask)
+        if len(dsts) == 1:
+            rid, pid = topo.addr(cores[dsts[0]], core)
+            g.remote_dma(T[dst_buf][:], T[buf][:], T.sem["a_" + dst_buf], T.sem.sent, pid, rid, mask)
+            return
+        ids = []
+        for d in dsts:
+            rid, pid = topo.addr(cores[d], core)
+            ids.append(DstId(rid=rid, pnc=pid))
+        g.remote_dma_fused([RemoteDMATransfer(dst_ids=ids, dma_engine_mask=mask, remote_sem=T.sem["a_" + dst_buf],
+                                              srcs=[T[buf][:]], dsts=[T[dst_buf][:] for _ in dsts], alu_op=0)],
+                           local_sem=T.sem.sent)
+
+    def store(buf):
+        need("s", [buf])
+        g.sync.dma_start(T.y[:], T[buf][:]).then_inc(T.sem.st, 16)
+
+    if rank == 0:
+        load("s", "sm", T.m)
+        load("a", "sx", T.x)
+        mm("pout", "sm", "sx")
+        send("pout", "pin", [pa])
+        send("pout", "pin", [pb])
+        send("pout", "pin", [third, 1, 2])
+        store("pout")
+    elif rank == 1:
+        load("s", "smt", T.mt)
+        load("a", "sm", T.m)
+        send("smt", "L1", [pa])
+        send("smt", "L1", [pb])
+        send("smt", "L1", [third, 2])
+        expect("pin", 0)
+        mm("yb", "sm", "pin")
+        store("yb")
+    elif rank == 2:
+        load("s", "sm", T.m)
+        send("sm", "L2", [pa])
+        send("sm", "L2", [pb])
+        send("sm", "L2", [third])
+        expect("L1", 1)
+        expect("pin", 0)
+        mm("t0", "L1", "sm")
+        mm("yb", "t0", "pin")
+        store("yb")
+    elif rank == third:
+        load("s", "smt", T.mt)
+        load("a", "sm", T.m)
+        send("smt", "L3", [pa])
+        send("smt", "L3", [pb])
+        for b, s in (("L1", 1), ("L2", 2), ("L4", pb), ("L5", pa), ("pin", 0)):
+            expect(b, s)
+        mm("t0", "L4", "L5")
+        mm("t1", "t0", "smt")
+        send("t1", "LB", [fa])
+        mm("t2", "L2", "L1")
+        mm("t3", "t2", "sm")
+        mm("yb", "t3", "pin")
+        store("yb")
+    elif rank == pb:
+        load("s", "smt", T.mt)
+        load("a", "sm", T.m)
+        send("smt", "L4", [pa])
+        send("smt", "L4", [third])
+        for b, s in (("L1", 1), ("L2", 2), ("L3", third), ("L5", pa), ("pin", 0)):
+            expect(b, s)
+        mm("t0", "smt", "L5")
+        mm("t1", "L3", "t0")
+        mm("t2", "L2", "L1")
+        mm("t3", "t2", "t1")
+        mm("t4", "L3", "sm")
+        mm("t5", "t2", "t4")
+        mm("pout", "t3", "pin")
+        send("pout", "pin", [fc])
+        mm("yb", "t5", "pin")
+        store("yb")
+    elif rank == pa:
+        load("s", "sm", T.m)
+        send("sm", "L5", [pb])
+        send("sm", "L5", [third])
+        for b, s in (("L1", 1), ("L2", 2), ("L3", third), ("L4", pb), ("pin", 0)):
+            expect(b, s)
+        mm("t0", "L1", "L2")
+        mm("t1", "L4", "sm")
+        mm("t2", "L3", "t1")
+        mm("pout", "t0", "pin")
+        send("pout", "pin", [fa])
+        mm("yb", "t2", "pout")
+        send("yb", "pin", [fb])
+        store("yb")
+    else:
+        later = [f for f in far if f > rank]
+        load("s", "sm", T.m)
+        if later:
+            load("a", "smt", T.mt)
+            send("smt", "L%d" % rank, later)
+        cur, k = "sm", 0
+        for j in reversed([f for f in far if f < rank]):
+            expect("L%d" % j, j)
+            mm("t%d" % k, "L%d" % j, cur)
+            cur, k = "t%d" % k, k + 1
+        if rank == fa:
+            expect("LB", third)
+            mm("t%d" % k, "LB", cur)
+            cur = "t%d" % k
+        expect("pin", pb if rank == fc else pa)
+        mm("yb", cur, "pin")
+        store("yb")
+
+    g.sync.wait_ge(T.sem.st, 16)
+    if cnt["sent"]:
+        g.wait_ge(T.sem.sent, cnt["sent"])

@@ -5,7 +5,6 @@ _B = "bfloat16"
 SCRATCH = {
     "sm": ("sbuf", [128, 128], _B), "smt": ("sbuf", [128, 128], _B), "sx": ("sbuf", [128, F], _B),
     "pin": ("sbuf", [128, F], _B), "pout": ("sbuf", [128, F], _B), "yb": ("sbuf", [128, F], _B),
-    "LB": ("sbuf", [128, 128], _B),
 }
 for _j in range(1, 8):
     SCRATCH["L%d" % _j] = ("sbuf", [128, 128], _B)
@@ -14,8 +13,9 @@ for _j in range(6):
 for _j in range(8):
     SCRATCH["ps%d" % _j] = ("psum", [128, 512], "float32")
 
-SEMAPHORES = (["ld_sm", "ld_smt", "ld_sx", "a_pin", "a_LB", "sent", "st"] + ["a_L%d" % j for j in range(1, 8)]
-              + ["q%d" % j for j in range(8)] + ["c%d" % j for j in range(8)])
+_NS = 12
+SEMAPHORES = (["ld_sm", "ld_smt", "ld_sx", "a_pin", "sent", "st"] + ["a_L%d" % j for j in range(1, 8)]
+              + ["q%d" % j for j in range(_NS)] + ["c%d" % j for j in range(_NS)])
 
 
 def rank_program(g, core, T, topo):
@@ -26,14 +26,13 @@ def rank_program(g, core, T, topo):
     n = len(cores)
     far = [r for r in range(1, n) if not topo.may_write(cores[0], cores[r])]
     mid = [r for r in range(1, n) if r not in far and all(topo.may_write(cores[r], cores[f]) for f in far)]
-    third, pb, pa = mid[0], mid[1], mid[2]
+    own = [r for r in range(1, n) if r not in far and r not in mid]
 
-    def partner(r):
-        return [f for f in far if topo.chip(cores[f]) == topo.chip(cores[r])][0]
-    fa, fb, fc = partner(third), partner(pa), partner(pb)
+    def partner(r, group):
+        return [f for f in group if topo.chip(cores[f]) == topo.chip(cores[r])][0]
 
     Q = {"g": g, "t": g.tensor, "v": g.vector, "s": g.sync, "a": g.scalar}
-    seen, ready, cnt = {}, {}, {"mm": 0, "sent": 0}
+    seen, ready, cnt = {}, {}, {"mm": 0, "bank": 0, "sent": 0}
 
     def need(q, bufs):
         for b in bufs:
@@ -56,12 +55,17 @@ def rank_program(g, core, T, topo):
         k = cnt["mm"]
         cnt["mm"] += 1
         w = T[rhs].shape[1]
-        ps = T["ps%d" % k]
+        parts = 2 if w > 128 else 1
+        h = w // parts
         need("t", [lhsT, rhs])
-        g.tensor.matmul(ps[:, 0:w], T[lhsT][:], T[rhs][:], start=True, stop=True).then_inc(T.sem["q%d" % k], 1)
-        g.vector.wait_ge(T.sem["q%d" % k], 1)
-        g.vector.tensor_copy(T[out][:], ps[:, 0:w]).then_inc(T.sem["c%d" % k], 1)
-        ready[out] = ("c%d" % k, 1)
+        for i in range(parts):
+            ps = T["ps%d" % (cnt["bank"] % 8)]
+            cnt["bank"] += 1
+            g.tensor.matmul(ps[:, 0:h], T[lhsT][:], T[rhs][:, i * h:(i + 1) * h], start=True, stop=True).then_inc(
+                T.sem["q%d" % k], 1)
+            g.vector.wait_ge(T.sem["q%d" % k], i + 1)
+            g.vector.tensor_copy(T[out][:, i * h:(i + 1) * h], ps[:, 0:h]).then_inc(T.sem["c%d" % k], 1)
+        ready[out] = ("c%d" % k, parts)
 
     def send(buf, dst_buf, dsts):
         need("g", [buf])
@@ -86,94 +90,88 @@ def rank_program(g, core, T, topo):
         g.sync.dma_start(T.y[:], T[buf][:]).then_inc(T.sem.st, 16)
 
     if rank == 0:
-        load("s", "sm", T.m)
         load("a", "sx", T.x)
+        load("s", "sm", T.m)
         mm("pout", "sm", "sx")
-        send("pout", "pin", [pa])
-        send("pout", "pin", [pb])
-        send("pout", "pin", [third, 1, 2])
+        send("pout", "pin", mid)
+        send("pout", "pin", own)
         store("pout")
-    elif rank == 1:
+    elif rank == own[0]:
         load("s", "smt", T.mt)
         load("a", "sm", T.m)
-        send("smt", "L1", [pa])
-        send("smt", "L1", [pb])
-        send("smt", "L1", [third, 2])
+        send("smt", "L1", mid)
+        send("smt", "L1", [own[1]])
         expect("pin", 0)
         mm("yb", "sm", "pin")
         store("yb")
-    elif rank == 2:
+    elif rank == own[1]:
         load("s", "sm", T.m)
-        send("sm", "L2", [pa])
-        send("sm", "L2", [pb])
-        send("sm", "L2", [third])
-        expect("L1", 1)
+        send("sm", "L2", mid)
+        expect("L1", own[0])
         expect("pin", 0)
         mm("t0", "L1", "sm")
         mm("yb", "t0", "pin")
         store("yb")
-    elif rank == third:
-        load("s", "smt", T.mt)
-        load("a", "sm", T.m)
-        send("smt", "L3", [pa])
-        send("smt", "L3", [pb])
-        for b, s in (("L1", 1), ("L2", 2), ("L4", pb), ("L5", pa), ("pin", 0)):
-            expect(b, s)
-        mm("t0", "L4", "L5")
-        mm("t1", "t0", "smt")
-        send("t1", "LB", [fa])
-        mm("t2", "L2", "L1")
-        mm("t3", "t2", "sm")
-        mm("yb", "t3", "pin")
-        store("yb")
-    elif rank == pb:
-        load("s", "smt", T.mt)
-        load("a", "sm", T.m)
-        send("smt", "L4", [pa])
-        send("smt", "L4", [third])
-        for b, s in (("L1", 1), ("L2", 2), ("L3", third), ("L5", pa), ("pin", 0)):
-            expect(b, s)
-        mm("t0", "smt", "L5")
-        mm("t1", "L3", "t0")
-        mm("t2", "L2", "L1")
-        mm("t3", "t2", "t1")
-        mm("t4", "L3", "sm")
-        mm("t5", "t2", "t4")
-        mm("pout", "t3", "pin")
-        send("pout", "pin", [fc])
-        mm("yb", "t5", "pin")
-        store("yb")
-    elif rank == pa:
-        load("s", "sm", T.m)
-        send("sm", "L5", [pb])
-        send("sm", "L5", [third])
-        for b, s in (("L1", 1), ("L2", 2), ("L3", third), ("L4", pb), ("pin", 0)):
-            expect(b, s)
+    elif rank in mid:
+        a, b, c = mid
+        fa, fb, fc = partner(a, far), partner(b, far), partner(c, far)
+        for j in own:
+            expect("L%d" % j, j)
+        expect("pin", 0)
+        if rank == a:
+            load("s", "smt", T.mt)
+            load("a", "sm", T.m)
+            send("smt", "L%d" % a, [fa, b, c])
+        elif rank == b:
+            load("s", "sm", T.m)
+            send("sm", "L%d" % b, [fb, c])
+        else:
+            load("s", "smt", T.mt)
+            load("a", "sm", T.m)
+            send("smt", "L%d" % c, [fc, fb])
         mm("t0", "L1", "L2")
-        mm("t1", "L4", "sm")
-        mm("t2", "L3", "t1")
         mm("pout", "t0", "pin")
-        send("pout", "pin", [fa])
-        mm("yb", "t2", "pout")
-        send("yb", "pin", [fb])
+        send("pout", "pin", [partner(rank, far)])
+        if rank == a:
+            mm("yb", "sm", "pout")
+        elif rank == b:
+            expect("L%d" % a, a)
+            mm("t1", "L%d" % a, "sm")
+            mm("yb", "t1", "pout")
+        else:
+            expect("L%d" % a, a)
+            expect("L%d" % b, b)
+            mm("t1", "L%d" % b, "L%d" % a)
+            mm("t2", "t1", "sm")
+            mm("yb", "t2", "pout")
         store("yb")
     else:
+        a, b, c = mid
+        fa, fb, fc = partner(a, far), partner(b, far), partner(c, far)
+        La, Lb, Lc = "L%d" % a, "L%d" % b, "L%d" % c
         later = [f for f in far if f > rank]
         load("s", "sm", T.m)
         if later:
             load("a", "smt", T.mt)
             send("smt", "L%d" % rank, later)
+        expect(La, a if rank == fa else fa)
+        expect(Lb, b if rank == fb else fb)
+        expect(Lc, c if rank in (fc, fb) else fb)
+        if rank == fa:
+            send(La, La, [fb, fc])
+        elif rank == fb:
+            send(Lc, Lc, [fa])
+            send(Lb, Lb, [fa, fc])
         cur, k = "sm", 0
         for j in reversed([f for f in far if f < rank]):
             expect("L%d" % j, j)
             mm("t%d" % k, "L%d" % j, cur)
             cur, k = "t%d" % k, k + 1
-        if rank == fa:
-            expect("LB", third)
-            mm("t%d" % k, "LB", cur)
-            cur = "t%d" % k
-        expect("pin", pb if rank == fc else pa)
-        mm("yb", cur, "pin")
+        mm("t%d" % k, Lc, cur)
+        mm("t%d" % (k + 1), Lb, La)
+        mm("t%d" % (k + 2), "t%d" % (k + 1), "t%d" % k)
+        expect("pin", partner(rank, mid))
+        mm("yb", "t%d" % (k + 2), "pin")
         store("yb")
 
     g.sync.wait_ge(T.sem.st, 16)

@@ -1,20 +1,25 @@
 from concourse.bass import DstId, RemoteDMATransfer
 
 F = 256
+H = 128
+BLK = 64
 _B = "bfloat16"
 SCRATCH = {
-    "sm": ("sbuf", [128, 128], _B), "smt": ("sbuf", [128, 128], _B), "sx": ("sbuf", [128, F], _B),
+    "sm": ("sbuf", [128, H], _B), "sx": ("sbuf", [128, F], _B),
     "pin": ("sbuf", [128, F], _B), "pout": ("sbuf", [128, F], _B), "yb": ("sbuf", [128, F], _B),
+    "ds": ("dram", [128, H], _B),
+    "dl0": ("dram", [128, H], _B),
 }
-for _j in range(1, 8):
-    SCRATCH["L%d" % _j] = ("sbuf", [128, 128], _B)
+for _j in range(0, 8):
+    SCRATCH["L%d" % _j] = ("sbuf", [128, H], _B)
 for _j in range(6):
-    SCRATCH["t%d" % _j] = ("sbuf", [128, 128], _B)
+    SCRATCH["t%d" % _j] = ("sbuf", [128, H], _B)
 for _j in range(8):
     SCRATCH["ps%d" % _j] = ("psum", [128, 512], "float32")
 
 _NS = 12
-SEMAPHORES = (["ld_sm", "ld_smt", "ld_sx", "a_pin", "sent", "st"] + ["a_L%d" % j for j in range(1, 8)]
+SEMAPHORES = (["ld_sm", "ld_sx", "ld_ds", "ld_L0", "a_dl0", "a_pin", "a_pin0", "a_pin1", "sent", "sentp", "st0", "st1"]
+              + ["a_L%d" % j for j in range(1, 8)]
               + ["q%d" % j for j in range(_NS)] + ["c%d" % j for j in range(_NS)])
 
 
@@ -32,14 +37,28 @@ def rank_program(g, core, T, topo):
         return [f for f in group if topo.chip(cores[f]) == topo.chip(cores[r])][0]
 
     Q = {"g": g, "t": g.tensor, "v": g.vector, "s": g.sync, "a": g.scalar}
-    seen, ready, cnt = {}, {}, {"mm": 0, "bank": 0, "sent": 0}
+    seen, ready, owner = {}, {}, {}
+    cnt = {"mm": 0, "bank": 0, "sent": 0, "sentp": 0}
 
-    def need(q, bufs):
-        for b in bufs:
-            s, v = ready[b]
-            if seen.get((q, s), 0) < v:
-                Q[q].wait_ge(T.sem[s], v)
-                seen[(q, s)] = v
+    def span(name):
+        if ":" in name:
+            b, i = name.split(":")
+            return b, int(i) * H
+        return name, 0
+
+    def ap(name):
+        b, lo = span(name)
+        return T[b][:, lo:lo + H] if ":" in name else T[b][:]
+
+    def wait(q, s, v):
+        if seen.get((q, s), 0) < v:
+            Q[q].wait_ge(T.sem[s], v)
+            seen[(q, s)] = v
+
+    def need(q, names):
+        for b in names:
+            s, v = ready[b] if b in ready else ready[span(b)[0]]
+            wait(q, s, v)
 
     def engines(mask):
         return bin(mask).count("1")
@@ -48,120 +67,148 @@ def rank_program(g, core, T, topo):
         Q[q].dma_start(T[buf][:], src[:]).then_inc(T.sem["ld_" + buf], 16)
         ready[buf] = ("ld_" + buf, 16)
 
-    def expect(buf, src_rank):
-        ready[buf] = ("a_" + buf, engines(topo.mask(cores[src_rank], core)))
+    def expect(name, src_rank):
+        ready[name] = ("a_" + name.replace(":", ""), engines(topo.mask(cores[src_rank], core)))
 
     def mm(out, lhsT, rhs):
         k = cnt["mm"]
         cnt["mm"] += 1
-        w = T[rhs].shape[1]
-        parts = 2 if w > 128 else 1
-        h = w // parts
         need("t", [lhsT, rhs])
+        ob, olo = span(out)
+        rb, rlo = span(rhs)
+        parts = H // BLK
         for i in range(parts):
-            ps = T["ps%d" % (cnt["bank"] % 8)]
+            bank = cnt["bank"] % 8
             cnt["bank"] += 1
-            g.tensor.matmul(ps[:, 0:h], T[lhsT][:], T[rhs][:, i * h:(i + 1) * h], start=True, stop=True).then_inc(
-                T.sem["q%d" % k], 1)
+            if bank in owner:
+                wait("t", owner[bank][0], owner[bank][1])
+            ps = T["ps%d" % bank]
+            g.tensor.matmul(ps[:, 0:BLK], T[lhsT][:], T[rb][:, rlo + i * BLK:rlo + (i + 1) * BLK],
+                            start=True, stop=True).then_inc(T.sem["q%d" % k], 1)
             g.vector.wait_ge(T.sem["q%d" % k], i + 1)
-            g.vector.tensor_copy(T[out][:, i * h:(i + 1) * h], ps[:, 0:h]).then_inc(T.sem["c%d" % k], 1)
+            g.vector.tensor_copy(T[ob][:, olo + i * BLK:olo + (i + 1) * BLK], ps[:, 0:BLK]).then_inc(
+                T.sem["c%d" % k], 1)
+            owner[bank] = ("c%d" % k, parts)
         ready[out] = ("c%d" % k, parts)
 
-    def send(buf, dst_buf, dsts):
-        need("g", [buf])
+    def send(src, dst, dsts, lsem="sent"):
+        need("g", [src])
         mask = topo.mask(core, cores[dsts[0]])
         for d in dsts:
             mask &= topo.mask(core, cores[d])
-        cnt["sent"] += engines(mask)
+        cnt[lsem] += engines(mask)
+        rsem = T.sem["a_" + dst.replace(":", "")]
         if len(dsts) == 1:
             rid, pid = topo.addr(cores[dsts[0]], core)
-            g.remote_dma(T[dst_buf][:], T[buf][:], T.sem["a_" + dst_buf], T.sem.sent, pid, rid, mask)
+            g.remote_dma(ap(dst), ap(src), rsem, T.sem[lsem], pid, rid, mask)
             return
         ids = []
         for d in dsts:
             rid, pid = topo.addr(cores[d], core)
             ids.append(DstId(rid=rid, pnc=pid))
-        g.remote_dma_fused([RemoteDMATransfer(dst_ids=ids, dma_engine_mask=mask, remote_sem=T.sem["a_" + dst_buf],
-                                              srcs=[T[buf][:]], dsts=[T[dst_buf][:] for _ in dsts], alu_op=0)],
-                           local_sem=T.sem.sent)
+        g.remote_dma_fused([RemoteDMATransfer(dst_ids=ids, dma_engine_mask=mask, remote_sem=rsem,
+                                              srcs=[ap(src)], dsts=[ap(dst) for _ in dsts], alu_op=0)],
+                           local_sem=T.sem[lsem])
 
     def store(buf):
-        need("s", [buf])
-        g.sync.dma_start(T.y[:], T[buf][:]).then_inc(T.sem.st, 16)
+        for i, q in enumerate(("s", "a")):
+            need(q, ["%s:%d" % (buf, i)])
+            if cnt["sentp"]:
+                wait(q, "sentp", cnt["sentp"])
+            Q[q].dma_start(T.y[:, i * H:(i + 1) * H], ap("%s:%d" % (buf, i))).then_inc(T.sem["st%d" % i], 16)
+
+    def apply(out, fac, src):
+        for i in range(2):
+            mm("%s:%d" % (out, i), fac, "%s:%d" % (src, i))
+
+    def take_mt0():
+        expect("dl0", 0)
+        need("a", ["dl0"])
+        load("a", "L0", T.dl0)
 
     if rank == 0:
+        load("s", "ds", T.mt)
         load("a", "sx", T.x)
         load("s", "sm", T.m)
-        mm("pout", "sm", "sx")
-        send("pout", "pin", mid)
-        send("pout", "pin", own)
+        send("ds", "dl0", own)
+        for i in range(2):
+            mm("pout:%d" % i, "sm", "sx:%d" % i)
+            send("pout:%d" % i, "pin:%d" % i, mid, "sentp")
+        send("sx", "pin", own)
         store("pout")
     elif rank == own[0]:
-        load("s", "smt", T.mt)
+        load("s", "ds", T.mt)
         load("a", "sm", T.m)
-        send("smt", "L1", mid)
-        send("smt", "L1", [own[1]])
+        send("ds", "L1", mid)
+        send("ds", "L1", [own[1]])
+        take_mt0()
+        mm("t0", "L0", "sm")
         expect("pin", 0)
-        mm("yb", "sm", "pin")
+        apply("yb", "t0", "pin")
         store("yb")
     elif rank == own[1]:
-        load("s", "sm", T.m)
-        send("sm", "L2", mid)
+        load("s", "ds", T.m)
+        load("a", "sm", T.m)
+        send("ds", "L2", mid)
         expect("L1", own[0])
-        expect("pin", 0)
+        take_mt0()
         mm("t0", "L1", "sm")
-        mm("yb", "t0", "pin")
+        mm("t1", "L0", "t0")
+        expect("pin", 0)
+        apply("yb", "t1", "pin")
         store("yb")
     elif rank in mid:
         a, b, c = mid
         fa, fb, fc = partner(a, far), partner(b, far), partner(c, far)
+        La, Lb, Lc = "L%d" % a, "L%d" % b, "L%d" % c
         for j in own:
             expect("L%d" % j, j)
-        expect("pin", 0)
+        for i in range(2):
+            expect("pin:%d" % i, 0)
+        load("s", "ds", T.m if rank == b else T.mt)
+        load("a", "sm", T.m)
         if rank == a:
-            load("s", "smt", T.mt)
-            load("a", "sm", T.m)
-            send("smt", "L%d" % a, [fa, b, c])
+            send("ds", La, [fa, b, c])
         elif rank == b:
-            load("s", "sm", T.m)
-            send("sm", "L%d" % b, [fb, c])
+            send("ds", Lb, [fb, c])
         else:
-            load("s", "smt", T.mt)
-            load("a", "sm", T.m)
-            send("smt", "L%d" % c, [fc, fb])
+            send("ds", Lc, [fc, fb])
         mm("t0", "L1", "L2")
-        mm("pout", "t0", "pin")
-        send("pout", "pin", [partner(rank, far)])
+        for i in range(2):
+            mm("pout:%d" % i, "t0", "pin:%d" % i)
+            send("pout:%d" % i, "pin:%d" % i, [partner(rank, far)], "sentp")
         if rank == a:
-            mm("yb", "sm", "pout")
+            apply("yb", "sm", "pout")
         elif rank == b:
-            expect("L%d" % a, a)
-            mm("t1", "L%d" % a, "sm")
-            mm("yb", "t1", "pout")
+            expect(La, a)
+            mm("t1", La, "sm")
+            apply("yb", "t1", "pout")
         else:
-            expect("L%d" % a, a)
-            expect("L%d" % b, b)
-            mm("t1", "L%d" % b, "L%d" % a)
+            expect(La, a)
+            expect(Lb, b)
+            mm("t1", Lb, La)
             mm("t2", "t1", "sm")
-            mm("yb", "t2", "pout")
+            apply("yb", "t2", "pout")
         store("yb")
     else:
         a, b, c = mid
         fa, fb, fc = partner(a, far), partner(b, far), partner(c, far)
         La, Lb, Lc = "L%d" % a, "L%d" % b, "L%d" % c
         later = [f for f in far if f > rank]
-        load("s", "sm", T.m)
         if later:
-            load("a", "smt", T.mt)
-            send("smt", "L%d" % rank, later)
+            load("s", "ds", T.mt)
+            load("a", "sm", T.m)
+            send("ds", "L%d" % rank, later)
+        else:
+            load("s", "sm", T.m)
         expect(La, a if rank == fa else fa)
         expect(Lb, b if rank == fb else fb)
         expect(Lc, c if rank in (fc, fb) else fb)
         if rank == fa:
             send(La, La, [fb, fc])
         elif rank == fb:
-            send(Lc, Lc, [fa])
             send(Lb, Lb, [fa, fc])
+            send(Lc, Lc, [fa])
         cur, k = "sm", 0
         for j in reversed([f for f in far if f < rank]):
             expect("L%d" % j, j)
@@ -170,10 +217,12 @@ def rank_program(g, core, T, topo):
         mm("t%d" % k, Lc, cur)
         mm("t%d" % (k + 1), Lb, La)
         mm("t%d" % (k + 2), "t%d" % (k + 1), "t%d" % k)
-        expect("pin", partner(rank, mid))
-        mm("yb", "t%d" % (k + 2), "pin")
+        for i in range(2):
+            expect("pin:%d" % i, partner(rank, mid))
+        apply("yb", "t%d" % (k + 2), "pin")
         store("yb")
 
-    g.sync.wait_ge(T.sem.st, 16)
+    g.sync.wait_ge(T.sem.st0, 16)
+    g.scalar.wait_ge(T.sem.st1, 16)
     if cnt["sent"]:
         g.wait_ge(T.sem.sent, cnt["sent"])

from concourse.bass import DstId, RemoteDMATransfer

F = 256
H = 128
BLK = 64
_B = "bfloat16"
SCRATCH = {
    "sm": ("sbuf", [128, H], _B), "sx": ("sbuf", [128, F], _B),
    "pin": ("sbuf", [128, F], _B), "pout": ("sbuf", [128, F], _B), "yb": ("sbuf", [128, F], _B),
    "ds": ("dram", [128, H], _B),
    "dl0": ("dram", [128, H], _B),
}
for _j in range(0, 8):
    SCRATCH["L%d" % _j] = ("sbuf", [128, H], _B)
for _j in range(6):
    SCRATCH["t%d" % _j] = ("sbuf", [128, H], _B)
for _j in range(8):
    SCRATCH["ps%d" % _j] = ("psum", [128, 512], "float32")

_NS = 12
SEMAPHORES = (["ld_sm", "ld_sx", "ld_ds", "ld_L0", "a_dl0", "a_pin", "a_pin0", "a_pin1", "sent", "sentp", "st0", "st1"]
              + ["a_L%d" % j for j in range(1, 8)]
              + ["q%d" % j for j in range(_NS)] + ["c%d" % j for j in range(_NS)])


def rank_program(g, core, T, topo):
    rank = T.rank_of(core)
    if rank is None:
        return
    cores = list(T.cores)
    n = len(cores)
    far = [r for r in range(1, n) if not topo.may_write(cores[0], cores[r])]
    mid = [r for r in range(1, n) if r not in far and all(topo.may_write(cores[r], cores[f]) for f in far)]
    own = [r for r in range(1, n) if r not in far and r not in mid]

    def partner(r, group):
        return [f for f in group if topo.chip(cores[f]) == topo.chip(cores[r])][0]

    Q = {"g": g, "t": g.tensor, "v": g.vector, "s": g.sync, "a": g.scalar}
    seen, ready, owner = {}, {}, {}
    cnt = {"mm": 0, "bank": 0, "sent": 0, "sentp": 0}

    def span(name):
        if ":" in name:
            b, i = name.split(":")
            return b, int(i) * H
        return name, 0

    def ap(name):
        b, lo = span(name)
        return T[b][:, lo:lo + H] if ":" in name else T[b][:]

    def wait(q, s, v):
        if seen.get((q, s), 0) < v:
            Q[q].wait_ge(T.sem[s], v)
            seen[(q, s)] = v

    def need(q, names):
        for b in names:
            s, v = ready[b] if b in ready else ready[span(b)[0]]
            wait(q, s, v)

    def engines(mask):
        return bin(mask).count("1")

    def load(q, buf, src):
        Q[q].dma_start(T[buf][:], src[:]).then_inc(T.sem["ld_" + buf], 16)
        ready[buf] = ("ld_" + buf, 16)

    def expect(name, src_rank):
        ready[name] = ("a_" + name.replace(":", ""), engines(topo.mask(cores[src_rank], core)))

    def mm(out, lhsT, rhs):
        k = cnt["mm"]
        cnt["mm"] += 1
        need("t", [lhsT, rhs])
        ob, olo = span(out)
        rb, rlo = span(rhs)
        parts = H // BLK
        for i in range(parts):
            bank = cnt["bank"] % 8
            cnt["bank"] += 1
            if bank in owner:
                wait("t", owner[bank][0], owner[bank][1])
            ps = T["ps%d" % bank]
            g.tensor.matmul(ps[:, 0:BLK], T[lhsT][:], T[rb][:, rlo + i * BLK:rlo + (i + 1) * BLK],
                            start=True, stop=True).then_inc(T.sem["q%d" % k], 1)
            g.vector.wait_ge(T.sem["q%d" % k], i + 1)
            g.vector.tensor_copy(T[ob][:, olo + i * BLK:olo + (i + 1) * BLK], ps[:, 0:BLK]).then_inc(
                T.sem["c%d" % k], 1)
            owner[bank] = ("c%d" % k, parts)
        ready[out] = ("c%d" % k, parts)

    def send(src, dst, dsts, lsem="sent"):
        need("g", [src])
        mask = topo.mask(core, cores[dsts[0]])
        for d in dsts:
            mask &= topo.mask(core, cores[d])
        cnt[lsem] += engines(mask)
        rsem = T.sem["a_" + dst.replace(":", "")]
        if len(dsts) == 1:
            rid, pid = topo.addr(cores[dsts[0]], core)
            g.remote_dma(ap(dst), ap(src), rsem, T.sem[lsem], pid, rid, mask)
            return
        ids = []
        for d in dsts:
            rid, pid = topo.addr(cores[d], core)
            ids.append(DstId(rid=rid, pnc=pid))
        g.remote_dma_fused([RemoteDMATransfer(dst_ids=ids, dma_engine_mask=mask, remote_sem=rsem,
                                              srcs=[ap(src)], dsts=[ap(dst) for _ in dsts], alu_op=0)],
                           local_sem=T.sem[lsem])

    def store(buf):
        for i, q in enumerate(("s", "a")):
            need(q, ["%s:%d" % (buf, i)])
            if cnt["sentp"]:
                wait(q, "sentp", cnt["sentp"])
            Q[q].dma_start(T.y[:, i * H:(i + 1) * H], ap("%s:%d" % (buf, i))).then_inc(T.sem["st%d" % i], 16)

    def apply(out, fac, src):
        for i in range(2):
            mm("%s:%d" % (out, i), fac, "%s:%d" % (src, i))

    def take_mt0():
        expect("dl0", 0)
        need("a", ["dl0"])
        load("a", "L0", T.dl0)

    if rank == 0:
        load("s", "ds", T.mt)
        load("a", "sx", T.x)
        load("s", "sm", T.m)
        send("ds", "dl0", own)
        for i in range(2):
            mm("pout:%d" % i, "sm", "sx:%d" % i)
            send("pout:%d" % i, "pin:%d" % i, mid, "sentp")
        send("sx", "pin", own)
        store("pout")
    elif rank == own[0]:
        load("s", "ds", T.mt)
        load("a", "sm", T.m)
        send("ds", "L1", mid)
        send("ds", "L1", [own[1]])
        take_mt0()
        mm("t0", "L0", "sm")
        expect("pin", 0)
        apply("yb", "t0", "pin")
        store("yb")
    elif rank == own[1]:
        load("s", "ds", T.m)
        load("a", "sm", T.m)
        send("ds", "L2", mid)
        expect("L1", own[0])
        take_mt0()
        mm("t0", "L1", "sm")
        mm("t1", "L0", "t0")
        expect("pin", 0)
        apply("yb", "t1", "pin")
        store("yb")
    elif rank in mid:
        a, b, c = mid
        fa, fb, fc = partner(a, far), partner(b, far), partner(c, far)
        La, Lb, Lc = "L%d" % a, "L%d" % b, "L%d" % c
        for j in own:
            expect("L%d" % j, j)
        for i in range(2):
            expect("pin:%d" % i, 0)
        load("s", "ds", T.m if rank == b else T.mt)
        load("a", "sm", T.m)
        if rank == a:
            send("ds", La, [fa, b, c])
        elif rank == b:
            send("ds", Lb, [fb, c])
        else:
            send("ds", Lc, [fc, fb])
        mm("t0", "L1", "L2")
        for i in range(2):
            mm("pout:%d" % i, "t0", "pin:%d" % i)
            send("pout:%d" % i, "pin:%d" % i, [partner(rank, far)], "sentp")
        if rank == a:
            apply("yb", "sm", "pout")
        elif rank == b:
            expect(La, a)
            mm("t1", La, "sm")
            apply("yb", "t1", "pout")
        else:
            expect(La, a)
            expect(Lb, b)
            mm("t1", Lb, La)
            mm("t2", "t1", "sm")
            apply("yb", "t2", "pout")
        store("yb")
    else:
        a, b, c = mid
        fa, fb, fc = partner(a, far), partner(b, far), partner(c, far)
        La, Lb, Lc = "L%d" % a, "L%d" % b, "L%d" % c
        later = [f for f in far if f > rank]
        if later:
            load("s", "ds", T.mt)
            load("a", "sm", T.m)
            send("ds", "L%d" % rank, later)
        else:
            load("s", "sm", T.m)
        expect(La, a if rank == fa else fa)
        expect(Lb, b if rank == fb else fb)
        expect(Lc, c if rank in (fc, fb) else fb)
        if rank == fa:
            send(La, La, [fb, fc])
        elif rank == fb:
            send(Lb, Lb, [fa, fc])
            send(Lc, Lc, [fa])
        cur, k = "sm", 0
        for j in reversed([f for f in far if f < rank]):
            expect("L%d" % j, j)
            mm("t%d" % k, "L%d" % j, cur)
            cur, k = "t%d" % k, k + 1
        mm("t%d" % k, Lc, cur)
        mm("t%d" % (k + 1), Lb, La)
        mm("t%d" % (k + 2), "t%d" % (k + 1), "t%d" % k)
        for i in range(2):
            expect("pin:%d" % i, partner(rank, mid))
        apply("yb", "t%d" % (k + 2), "pin")
        store("yb")

    g.sync.wait_ge(T.sem.st0, 16)
    g.scalar.wait_ge(T.sem.st1, 16)
    if cnt["sent"]:
        g.wait_ge(T.sem.sent, cnt["sent"])
